import numpy as np
import ml_dtypes


def mxq(x, axis, fmt="e4m3"):
    dtype, down = {"e4m3": (ml_dtypes.float8_e4m3fn, 7), "e5m2": (ml_dtypes.float8_e5m2, 14)}[fmt]
    v = np.moveaxis(np.asarray(x, np.float32).astype(ml_dtypes.bfloat16).astype(np.float64), axis, -1)
    blocks = v.reshape(v.shape[:-1] + (-1, 32))
    amax = np.abs(blocks).max(-1, keepdims=True)
    byte = np.maximum(np.where(amax > 0, np.frexp(amax)[1] - 1 + 127, 0) - down, 1)
    scale = np.exp2(byte - 127.0)
    codes = (blocks / scale).astype(np.float32).astype(dtype).astype(np.float64)
    return np.moveaxis((codes * scale).reshape(v.shape), -1, axis)


WIDE = False


def mx_kscale(k):
    if not WIDE:
        return np.ones(k)
    levels = np.array([10, -10, 5, -5, 0])
    if k % 512:
        return np.exp2(np.random.permutation(np.resize(levels, k // 32))).repeat(32)
    a = np.empty((k // 512, 16))
    for p in range(k // 512):
        a[p, :8] = np.random.permutation(np.resize(levels, 8))
        for g in range(8):
            far = levels[np.abs(levels - a[p, g]) >= 10]
            a[p, g + 8] = far[np.random.randint(len(far))]
    return np.exp2(a.ravel()).repeat(32)


def f64(x):
    return np.asarray(x).astype(np.float64)


def striped(idx):
    return np.tile(idx.reshape(-1, 16).T, (8, 1)).astype(np.uint16)


def unstriped(offs):
    return offs[:16].T.reshape(-1).astype(np.int64)


def pack_weight(w):
    k, n = w.shape
    w = f64(np.asarray(w, np.float32).astype(ml_dtypes.bfloat16)).reshape(k // 32, 32, n)
    amax = np.abs(w).max(1)
    byte = np.clip(np.where(amax > 0, np.frexp(amax)[1] - 1 + 127 - 7, 1), 1, 254)
    scaled = (w * np.exp2(127.0 - byte)[:, None, :]).reshape(k, n).astype(np.float32)
    words = np.ascontiguousarray(scaled.reshape(k // 512, 128, 4, n).transpose(0, 1, 3, 2)).astype(ml_dtypes.float8_e4m3fn).view(np.uint8)
    return words, np.ascontiguousarray(byte.astype(np.uint8).reshape(k // 512, 16, n))


def unpack_weight(words, scales):
    g, p, n, _ = words.shape
    vals = np.ascontiguousarray(words).view(ml_dtypes.float8_e4m3fn).astype(np.float64) * np.repeat(np.exp2(scales.astype(np.float64) - 127.0), 8, axis=1)[..., None]
    return vals.transpose(0, 1, 3, 2).reshape(g * 512, n)


def relu(v):
    return np.maximum(v, 0.0)


K, T, S, H, N = 1024, 2048, 1024, 512, 128
P = 2 ** 7


def setup_inputs():
    n = np.random.standard_normal
    s = mx_kscale(K)[:, None]
    u = mx_kscale(H)
    packed_xT = pack_weight(n((K, T)) * s)
    return {
        "x_words": packed_xT[0],
        "x_scales": packed_xT[1],
        "w1": (n((K, H)) / np.sqrt(K) / s * u).astype(np.float32),
        "w2": (n((H, N)) / np.sqrt(H) / u[:, None]).astype(np.float32),
        "share": np.tile(np.random.uniform(0.1, 0.9, S), (P, 1)).astype(np.float32),
        "offs": striped(np.random.permutation(T)[:S]),
        "par": striped(np.random.permutation(S)[(S * np.random.uniform(0, 1, S) ** 4).astype(np.int64)]),
    }


def reference(x_words, x_scales, w1, w2, share, offs, par):
    xq = unpack_weight(x_words, x_scales)[:, unstriped(offs)]
    h = relu(mxq(f64(w1), 0, "e4m3").T @ xq)
    z = h + h[:, unstriped(par)] * f64(share)[:1]
    return mxq(f64(w2), 0, "e4m3").T @ mxq(z, 0, "e4m3")

@@ -1,0 +1,206 @@
+from contextlib import ExitStack
+
+import concourse.mybir as mybir
+from concourse.masks import make_identity
+
+K, T, S, H, N = 1024, 2048, 1024, 512, 128
+FLOPS = 2 * K * H * S + 2 * H * N * S
+
+F32 = mybir.dt.float32
+BF16 = mybir.dt.bfloat16
+I32 = mybir.dt.int32
+U32 = mybir.dt.uint32
+U16 = mybir.dt.uint16
+U8 = mybir.dt.uint8
+FP8X4 = mybir.dt.float8_e4m3fn_x4
+RELU = mybir.ActivationFunctionType.Relu
+MULT = mybir.AluOpType.mult
+
+P = 128
+PACK = 4
+PASSES = K // (P * PACK)
+PLANES = H // P
+HALF = S // 2
+BANKS = 8
+GROUPS = [(0, 256), (256, 256), (512, 256), (768, 128), (896, 128)]
+
+
+def tile_picked_treeup_relu_p_kernel(
+    tc, x_words, x_scales, w1, w2, share, offs, par, out
+):
+    nc = tc.nc
+    with ExitStack() as ctx:
+        keep = ctx.enter_context(tc.tile_pool(name="keep", bufs=1))
+        psum = ctx.enter_context(tc.psum_pool(name="psum", bufs=1))
+        turn = [0]
+
+        def next_bank(shape, name):
+            t = psum.tile(shape, F32, name=name, tag=f"bank{turn[0] % BANKS}")
+            turn[0] = turn[0] + 1
+            return t
+
+        offs_t = keep.tile([P, S // 16], U16, name="offs_t")
+        par_t = keep.tile([P, S // 16], U16, name="par_t")
+        xs = keep.tile([P, T], U8, name="xs", align_bytes=64)
+        xw = [keep.tile([P, T], I32, name=f"xw{z}", align_bytes=64) for z in range(PASSES)]
+        share_t = keep.tile([P, S], F32, name="share_t")
+        w1_raw = [[keep.tile([P, PACK, P], F32, name=f"w1r{a}{z}") for z in range(PASSES)] for a in range(PLANES)]
+        w2_raw = keep.tile([P, PACK, N], F32, name="w2_raw")
+        ident = keep.tile([P, P], F32, name="ident")
+        warm = keep.tile([P, 8], F32, name="warm")
+
+        def load_w1(a, z):
+            rows = w1[z * 512 : (z + 1) * 512, a * P : (a + 1) * P]
+            nc.sync.dma_start(out=w1_raw[a][z][:], in_=rows.rearrange("(p t) c -> p t c", t=PACK))
+
+        def load_x(z):
+            nc.sync.dma_start(out=xw[z][:], in_=x_words[z].rearrange("p c r -> p (c r)").bitcast(I32))
+
+        def load_w2():
+            nc.sync.dma_start(out=w2_raw[:], in_=w2.rearrange("(p t) m -> p t m", t=PACK))
+
+        nc.vector.memset(xs[:].bitcast(I32), 0)
+        nc.sync.dma_start(offs_t[:], offs)
+        load_w1(0, 0)
+        for q in range(4):
+            nc.sync.dma_start(
+                out=xs[32 * q : 32 * q + 8, :].bitcast(I32),
+                in_=x_scales[:, 4 * q : 4 * q + 4, :].bitcast(I32),
+            )
+        load_x(0)
+        load_w1(0, 1)
+        load_x(1)
+
+        for a in range(1, PLANES):
+            load_w1(a, 0)
+            load_w1(a, 1)
+            if a == 3:
+                nc.sync.dma_start(par_t[:], par)
+                nc.sync.dma_start(out=share_t[:], in_=share)
+        load_w2()
+
+        make_identity(nc, ident[:])
+        nc.scalar.activation(warm[:, 0:1], ident[:, 0:1], RELU)
+
+        gs = keep.tile([P, S], U8, name="gs", align_bytes=64)
+        nc.vector.tensor_copy(gs[:], xs[:].indirect(offs_t[:]))
+        gw0 = keep.tile([P, S], U32, name="gw0", align_bytes=64)
+        nc.vector.tensor_copy(gw0[:], xw[0][:].bitcast(U32).indirect(offs_t[:]))
+
+        w1_codes = [keep.tile([P, PASSES * P], U32, name=f"w1c{a}", align_bytes=64) for a in range(PLANES)]
+        w1_scales = [keep.tile([P, PASSES * P], U8, name=f"w1s{a}", align_bytes=64) for a in range(PLANES)]
+
+        def prep_w1(a, copy):
+            wb = keep.tile([P, PASSES * P * PACK], BF16, name=f"wb{a}", align_bytes=64)
+            for z in range(PASSES):
+                copy(
+                    wb[:, z * 512 : (z + 1) * 512].rearrange("p (u m e t) -> p m t u e", u=2, m=32, e=2, t=PACK),
+                    w1_raw[a][z][:].rearrange("p t (m u e) -> p m t u e", m=32, u=2, e=2),
+                )
+            nc.vector.quantize_mx(out=w1_codes[a][:].bitcast(FP8X4), scales=w1_scales[a][:], in_=wb[:])
+
+        prep_w1(0, nc.scalar.copy)
+        gw1 = [keep.tile([P, HALF], U32, name=f"gw1{hf}", align_bytes=64) for hf in range(2)]
+        for hf in range(2):
+            nc.vector.tensor_copy(gw1[hf][:], xw[1][:].bitcast(U32).indirect(offs_t[:, hf * 32 : (hf + 1) * 32]))
+
+        h = []
+
+        def layer1(a):
+            h.append(keep.tile([P, S], F32, name=f"h{a}", tag=("w1r11" if a == 0 else f"h{a}")))
+            for hf in range(2):
+                cols = slice(hf * HALF, (hf + 1) * HALF)
+                acc = next_bank([P, HALF], f"acc{a}{hf}")
+                for z in range(PASSES):
+                    rhs = gw0[:, cols] if z == 0 else gw1[hf][:]
+                    nc.tensor.matmul_mx(
+                        out=acc[:],
+                        lhsT=w1_codes[a][:, z * P : (z + 1) * P].bitcast(FP8X4),
+                        lhsT_scale=w1_scales[a][:, z * P : (z + 1) * P],
+                        rhs=rhs.bitcast(FP8X4),
+                        rhs_scale=gs[4 * z : P, cols],
+                        start=(z == 0),
+                        stop=(z == PASSES - 1),
+                    )
+                nc.scalar.activation(h[a][:, cols], acc[:], RELU)
+
+        w2_codes = keep.tile([P, N], U32, name="w2c", align_bytes=64)
+        w2_scales = keep.tile([P, N], U8, name="w2s", align_bytes=64)
+
+        def prep_w2():
+            wb2 = keep.tile([P, N * PACK], BF16, name="w2b", align_bytes=64)
+            nc.scalar.copy(
+                wb2[:].rearrange("p (c i t) -> p c t i", i=4, t=PACK),
+                w2_raw[:].rearrange("p t (c i) -> p c t i", i=4),
+            )
+            nc.vector.quantize_mx(out=w2_codes[:].bitcast(FP8X4), scales=w2_scales[:], in_=wb2[:])
+
+        zt = [keep.tile([P, n // P, 2, 2 * P], BF16, name=f"zt{j0}", align_bytes=64) for j0, n in GROUPS]
+
+        def piece(a, j0, n):
+            g = keep.tile([P, n], F32, name=f"g{a}_{j0}")
+            nc.vector.tensor_tensor(
+                g[:], h[a][:].indirect(par_t[:, j0 // 16 : (j0 + n) // 16]), share_t[:, j0 : j0 + n], MULT
+            )
+            bank = next_bank([P, n // P, P], f"ta{a}_{j0}")
+            blocks = n // P
+            for b in range(blocks):
+                nc.tensor.matmul(bank[:, b, :], h[a][:, j0 + b * P : j0 + (b + 1) * P], ident[:],
+                                 start=(b == 0), stop=False, is_transpose=True)
+            for b in range(blocks):
+                nc.tensor.matmul(bank[:, b, :], g[:, b * P : (b + 1) * P], ident[:],
+                                 start=False, stop=(b == blocks - 1), is_transpose=True)
+            for k, (g0, gn) in enumerate(GROUPS):
+                if j0 <= g0 < j0 + n:
+                    b0 = (g0 - j0) // P
+                    nc.scalar.copy(
+                        zt[k][:, :, :, 64 * a : 64 * (a + 1)],
+                        bank[:, b0 : b0 + gn // P, :].rearrange("p b (u x) -> p b u x", u=2),
+                    )
+
+        def turn_back(k, copy):
+            n = GROUPS[k][1]
+            words = zt[k][:].rearrange("p b u x -> p (b u x)").bitcast(F32)
+            bk = next_bank([P, 2, n], f"bk{k}")
+            for b in range(n // P):
+                for u in range(2):
+                    w0 = (2 * b + u) * P
+                    nc.tensor.transpose(bk[:, u, b * P : (b + 1) * P], words[:, w0 : w0 + P], ident[:])
+            zq = keep.tile([P, n * PACK], BF16, name=f"zq{k}", align_bytes=64)
+            copy(zq[:].bitcast(F32).rearrange("p (j u) -> p j u", u=2), bk[:].rearrange("p u j -> p j u"))
+            return zq
+
+        def layer2(k, zq, copy):
+            j0, n = GROUPS[k]
+            zc = keep.tile([P, n], U32, name=f"zc{k}", align_bytes=64)
+            zs = keep.tile([P, n], U8, name=f"zs{k}", align_bytes=64)
+            nc.vector.quantize_mx(out=zc[:].bitcast(FP8X4), scales=zs[:], in_=zq[:])
+            acc = next_bank([P, n], f"res{k}")
+            nc.tensor.matmul_mx(
+                out=acc[:], lhsT=w2_codes[:].bitcast(FP8X4), lhsT_scale=w2_scales[:],
+                rhs=zc[:].bitcast(FP8X4), rhs_scale=zs[:], start=True, stop=True,
+            )
+            res = keep.tile([P, n], F32, name=f"o{k}")
+            copy(res[:], acc[:])
+            nc.sync.dma_start(out=out[:, j0 : j0 + n], in_=res[:])
+
+        prep_w1(1, nc.scalar.copy)
+        layer1(0)
+        layer1(1)
+        prep_w1(2, nc.vector.tensor_copy)
+        layer1(2)
+        prep_w1(3, nc.vector.tensor_copy)
+        layer1(3)
+        prep_w2()
+        turn[0] = 6
+        zq = []
+        for hf in range(2):
+            for a in range(PLANES - 1):
+                piece(a, hf * HALF, HALF)
+            mine = [k for k, (j0, n) in enumerate(GROUPS) if j0 // HALF == hf]
+            for k in mine:
+                piece(PLANES - 1, *GROUPS[k])
+            for k in mine:
+                zq.append(turn_back(k, nc.scalar.copy))
+        for k in range(len(GROUPS)):
+            layer2(k, zq[k], nc.vector.tensor_copy)

@@ -15,6 +15,7 @@ U8 = mybir.dt.uint8
 FP8X4 = mybir.dt.float8_e4m3fn_x4
 RELU = mybir.ActivationFunctionType.Relu
 MULT = mybir.AluOpType.mult
+MAX = mybir.AluOpType.max
 
 P = 128
 PACK = 4
@@ -23,6 +24,13 @@ PLANES = H // P
 HALF = S // 2
 BANKS = 8
 GROUPS = [(0, 256), (256, 256), (512, 256), (768, 128), (896, 128)]
+UNITS = [(0, 256), (256, 256), (512, 256), (768, 128), (896, 128)]
+LOADS = [(0,1),(1,1),(2,1),(3,1)]
+ORDER = "x0 w00 x1 w01 w10 w11 r w20 w21 v w30 w31"
+GW1 = [(0, 512), (512, 256), (768, 256)]
+CAST = "SS SS VV SS V"
+TAGS = {"gw11": "wb01", "wb3": "g2", "zc0": "g3", "zc256": "g2"}
+GRING = 4
 
 
 def tile_picked_treeup_relu_p_kernel(
@@ -32,26 +40,28 @@ def tile_picked_treeup_relu_p_kernel(
     with ExitStack() as ctx:
         keep = ctx.enter_context(tc.tile_pool(name="keep", bufs=1))
         psum = ctx.enter_context(tc.psum_pool(name="psum", bufs=1))
-        turn = [0]
+        made = [0]
 
-        def next_bank(shape, name):
-            t = psum.tile(shape, F32, name=name, tag=f"bank{turn[0] % BANKS}")
-            turn[0] = turn[0] + 1
-            return t
+        def bank_tile(shape, name, b):
+            return psum.tile(shape, F32, name=name, tag=f"bank{b}")
+
+        def sb(shape, dtype, name):
+            return keep.tile(shape, dtype, name=name, align_bytes=64, tag=TAGS.get(name, name))
 
         offs_t = keep.tile([P, S // 16], U16, name="offs_t")
         par_t = keep.tile([P, S // 16], U16, name="par_t")
         xs = keep.tile([P, T], U8, name="xs", align_bytes=64)
         xw = [keep.tile([P, T], I32, name=f"xw{z}", align_bytes=64) for z in range(PASSES)]
-        share_t = keep.tile([P, S], F32, name="share_t")
-        w1_raw = [[keep.tile([P, PACK, P], F32, name=f"w1r{a}{z}") for z in range(PASSES)] for a in range(PLANES)]
-        w2_raw = keep.tile([P, PACK, N], F32, name="w2_raw")
+        w1_raw = {(a0, z): keep.tile([P, PACK, P * na], F32, name=f"w1r{a0}{z}", align_bytes=64)
+                  for a0, na in LOADS for z in range(PASSES)}
+        w2_raw = keep.tile([P, PACK, N], F32, name="w2_raw", align_bytes=64)
         ident = keep.tile([P, P], F32, name="ident")
         warm = keep.tile([P, 8], F32, name="warm")
 
-        def load_w1(a, z):
-            rows = w1[z * 512 : (z + 1) * 512, a * P : (a + 1) * P]
-            nc.sync.dma_start(out=w1_raw[a][z][:], in_=rows.rearrange("(p t) c -> p t c", t=PACK))
+        def load_w1(k, z):
+            a0, na = LOADS[k]
+            rows = w1[z * 512 : (z + 1) * 512, a0 * P : (a0 + na) * P]
+            nc.sync.dma_start(out=w1_raw[a0, z][:], in_=rows.rearrange("(p t) c -> p t c", t=PACK))
 
         def load_x(z):
             nc.sync.dma_start(out=xw[z][:], in_=x_words[z].rearrange("p c r -> p (c r)").bitcast(I32))
@@ -59,148 +69,318 @@ def tile_picked_treeup_relu_p_kernel(
         def load_w2():
             nc.sync.dma_start(out=w2_raw[:], in_=w2.rearrange("(p t) m -> p t m", t=PACK))
 
-        nc.vector.memset(xs[:].bitcast(I32), 0)
-        nc.sync.dma_start(offs_t[:], offs)
-        load_w1(0, 0)
-        for q in range(4):
-            nc.sync.dma_start(
-                out=xs[32 * q : 32 * q + 8, :].bitcast(I32),
-                in_=x_scales[:, 4 * q : 4 * q + 4, :].bitcast(I32),
-            )
-        load_x(0)
-        load_w1(0, 1)
-        load_x(1)
+        def load_scales():
+            for q in range(4):
+                nc.sync.dma_start(
+                    out=xs[32 * q : 32 * q + 8, :].bitcast(I32),
+                    in_=x_scales[:, 4 * q : 4 * q + 4, :].bitcast(I32),
+                )
 
-        for a in range(1, PLANES):
-            load_w1(a, 0)
-            load_w1(a, 1)
-            if a == 3:
+        nc.gpsimd.memset(xs[:].bitcast(I32), 0)
+        scol = keep.tile([P, 8], F32, name="scol")
+        nc.sync.dma_start(offs_t[:], offs)
+        if "r" in ORDER.split():
+            nc.sync.dma_start(out=scol[:], in_=share[0, :].rearrange("(p e) -> p e", e=8))
+        else:
+            nc.sync.dma_start(par_t[:], par)
+        load_scales()
+        for w in ORDER.split():
+            if w[0] == "x":
+                load_x(int(w[1]))
+            elif w[0] == "w":
+                load_w1(int(w[1]), int(w[2]))
+            elif w[0] == "r":
                 nc.sync.dma_start(par_t[:], par)
-                nc.sync.dma_start(out=share_t[:], in_=share)
-        load_w2()
+            else:
+                load_w2()
 
         make_identity(nc, ident[:])
         nc.scalar.activation(warm[:, 0:1], ident[:, 0:1], RELU)
+        ENG = {"S": nc.scalar.copy, "V": nc.vector.tensor_copy}
+        casts = CAST.split()
 
-        gs = keep.tile([P, S], U8, name="gs", align_bytes=64)
-        nc.vector.tensor_copy(gs[:], xs[:].indirect(offs_t[:]))
-        gw0 = keep.tile([P, S], U32, name="gw0", align_bytes=64)
-        nc.vector.tensor_copy(gw0[:], xw[0][:].bitcast(U32).indirect(offs_t[:]))
-
-        w1_codes = [keep.tile([P, PASSES * P], U32, name=f"w1c{a}", align_bytes=64) for a in range(PLANES)]
-        w1_scales = [keep.tile([P, PASSES * P], U8, name=f"w1s{a}", align_bytes=64) for a in range(PLANES)]
-
-        def prep_w1(a, copy):
-            wb = keep.tile([P, PASSES * P * PACK], BF16, name=f"wb{a}", align_bytes=64)
-            for z in range(PASSES):
-                copy(
-                    wb[:, z * 512 : (z + 1) * 512].rearrange("p (u m e t) -> p m t u e", u=2, m=32, e=2, t=PACK),
-                    w1_raw[a][z][:].rearrange("p t (m u e) -> p m t u e", m=32, u=2, e=2),
-                )
-            nc.vector.quantize_mx(out=w1_codes[a][:].bitcast(FP8X4), scales=w1_scales[a][:], in_=wb[:])
-
-        prep_w1(0, nc.scalar.copy)
-        gw1 = [keep.tile([P, HALF], U32, name=f"gw1{hf}", align_bytes=64) for hf in range(2)]
-        for hf in range(2):
-            nc.vector.tensor_copy(gw1[hf][:], xw[1][:].bitcast(U32).indirect(offs_t[:, hf * 32 : (hf + 1) * 32]))
-
-        h = []
-
-        def layer1(a):
-            h.append(keep.tile([P, S], F32, name=f"h{a}", tag=("w1r11" if a == 0 else f"h{a}")))
+        if "r" in ORDER.split():
+            whole = keep.tile([P, S], F32, name="share_w")
+            share_t = [whole[:, :HALF], whole[:, HALF:]]
             for hf in range(2):
-                cols = slice(hf * HALF, (hf + 1) * HALF)
-                acc = next_bank([P, HALF], f"acc{a}{hf}")
+                bank = bank_tile([P, HALF], f"sB{hf}", 5 + hf)
+                for c in range(4):
+                    b = 4 * hf + c
+                    nc.tensor.transpose(bank[:, c * P : (c + 1) * P], scol[:, b : b + 1].to_broadcast([P, P]), ident[:])
+                nc.scalar.copy(whole[:].rearrange("p (n e) -> p n e", e=8)[:, :, 4 * hf : 4 * hf + 4], bank[:].rearrange("p (e n) -> p n e", e=4))
+        gs = sb([P, S], U8, "gs")
+        gw0 = sb([P, S], U32, "gw0")
+        gw1 = {}
+        wb = {}
+        w1c = {}
+        w1s = {}
+        h = {}
+        acc = {}
+        zt = [sb([P, n // P, 2, 2 * P], BF16, f"zt{j0}") for j0, n in GROUPS]
+        zq = {j0: sb([P, n * PACK], BF16, f"zq{j0}") for j0, n in UNITS}
+        w2q = {}
+
+        def gather_x1(i):
+            j0, n = GW1[i]
+            gw1[i] = sb([P, n], U32, f"gw1{i}")
+            nc.vector.tensor_copy(gw1[i][:], xw[1][:].bitcast(U32).indirect(offs_t[:, j0 // 16 : (j0 + n) // 16]))
+
+        def cast_w1(a, z):
+            a0 = max(b for b, na in LOADS if b <= a)
+            if a == 0:
+                wb[a, z] = sb([P, 512], BF16, f"wb{a}{z}")[:]
+            else:
+                if z == 0:
+                    wb[a] = sb([P, 1024], BF16, f"wb{a}")
+                wb[a, z] = wb[a][:, z * 512 : (z + 1) * 512]
+            ENG[casts[a][z]](
+                wb[a, z].rearrange("p (u m e t) -> p m t u e", u=2, m=32, e=2, t=PACK),
+                w1_raw[a0, z][:, :, (a - a0) * P : (a - a0 + 1) * P].rearrange("p t (m u e) -> p m t u e", m=32, u=2, e=2),
+            )
+
+        def quant_w1(a, z):
+            if a == 0:
+                c = sb([P, P], U32, f"w1c{a}{z}")
+                s = sb([P, P], U8, f"w1s{a}{z}")
+                nc.vector.quantize_mx(out=c[:].bitcast(FP8X4), scales=s[:], in_=wb[a, z])
+                w1c[a, z], w1s[a, z] = c[:], s[:]
+            else:
+                c = sb([P, 2 * P], U32, f"w1c{a}")
+                s = sb([P, 2 * P], U8, f"w1s{a}")
+                nc.vector.quantize_mx(out=c[:].bitcast(FP8X4), scales=s[:], in_=wb[a][:])
+                for y in range(2):
+                    w1c[a, y], w1s[a, y] = c[:, y * P : (y + 1) * P], s[:, y * P : (y + 1) * P]
+
+        def mm1(a, i, b):
+            j0, n = GW1[i]
+            acc[a, i] = bank_tile([P, n], f"acc{a}{i}", b)
+            for z in range(PASSES):
+                rhs = gw0[:, j0 : j0 + n] if z == 0 else gw1[i][:]
+                nc.tensor.matmul_mx(
+                    out=acc[a, i][:], lhsT=w1c[a, z].bitcast(FP8X4), lhsT_scale=w1s[a, z],
+                    rhs=rhs.bitcast(FP8X4), rhs_scale=gs[4 * z : P, j0 : j0 + n],
+                    start=(z == 0), stop=(z == PASSES - 1),
+                )
+
+        def mm1pair(a, b):
+            bk = bank_tile([P, HALF], f"acc{a}1", b)
+            for i in (1, 2):
+                j0, n = GW1[i]
                 for z in range(PASSES):
-                    rhs = gw0[:, cols] if z == 0 else gw1[hf][:]
+                    rhs = gw0[:, j0 : j0 + n] if z == 0 else gw1[i][:]
                     nc.tensor.matmul_mx(
-                        out=acc[:],
-                        lhsT=w1_codes[a][:, z * P : (z + 1) * P].bitcast(FP8X4),
-                        lhsT_scale=w1_scales[a][:, z * P : (z + 1) * P],
-                        rhs=rhs.bitcast(FP8X4),
-                        rhs_scale=gs[4 * z : P, cols],
-                        start=(z == 0),
-                        stop=(z == PASSES - 1),
+                        out=bk[:, j0 - HALF : j0 - HALF + n], lhsT=w1c[a, z].bitcast(FP8X4), lhsT_scale=w1s[a, z],
+                        rhs=rhs.bitcast(FP8X4), rhs_scale=gs[4 * z : P, j0 : j0 + n],
+                        start=(z == 0), stop=(z == PASSES - 1),
                     )
-                nc.scalar.activation(h[a][:, cols], acc[:], RELU)
+            acc[a, 1] = bk
 
-        w2_codes = keep.tile([P, N], U32, name="w2c", align_bytes=64)
-        w2_scales = keep.tile([P, N], U8, name="w2s", align_bytes=64)
+        def relu(a, i, e):
+            if a not in h:
+                h[a] = sb([P, S], F32, f"h{a}")
+            j0 = GW1[i][0]
+            n = acc[a, i].shape[1]
+            if e == "S":
+                nc.scalar.activation(h[a][:, j0 : j0 + n], acc[a, i][:], RELU)
+            else:
+                nc.vector.tensor_scalar(h[a][:, j0 : j0 + n], acc[a, i][:], 0.0, None, MAX)
 
-        def prep_w2():
-            wb2 = keep.tile([P, N * PACK], BF16, name="w2b", align_bytes=64)
-            nc.scalar.copy(
-                wb2[:].rearrange("p (c i t) -> p c t i", i=4, t=PACK),
+        def cast_w2():
+            w2q["b"] = sb([P, N * PACK], BF16, "w2b")
+            ENG[casts[4]](
+                w2q["b"][:].rearrange("p (c i t) -> p c t i", i=4, t=PACK),
                 w2_raw[:].rearrange("p t (c i) -> p c t i", i=4),
             )
-            nc.vector.quantize_mx(out=w2_codes[:].bitcast(FP8X4), scales=w2_scales[:], in_=wb2[:])
 
-        zt = [keep.tile([P, n // P, 2, 2 * P], BF16, name=f"zt{j0}", align_bytes=64) for j0, n in GROUPS]
+        def quant_w2():
+            w2q["c"] = sb([P, N], U32, "w2c")
+            w2q["s"] = sb([P, N], U8, "w2s")
+            nc.vector.quantize_mx(out=w2q["c"][:].bitcast(FP8X4), scales=w2q["s"][:], in_=w2q["b"][:])
 
-        def piece(a, j0, n):
-            g = keep.tile([P, n], F32, name=f"g{a}_{j0}")
+        gt = {}
+        ta = {}
+        bks = {}
+        zcs = {}
+        ress = {}
+
+        def gath(a, j0, n):
+            g = keep.tile([P, n], F32, name=f"g{a}_{j0}", align_bytes=64, tag=TAGS.get(f"g{a}_{j0}", f"g{made[0] % GRING}"))
+            made[0] = made[0] + 1
             nc.vector.tensor_tensor(
-                g[:], h[a][:].indirect(par_t[:, j0 // 16 : (j0 + n) // 16]), share_t[:, j0 : j0 + n], MULT
+                g[:], h[a][:].indirect(par_t[:, j0 // 16 : (j0 + n) // 16]),
+                share_t[j0 // HALF][:, j0 % HALF : j0 % HALF + n], MULT
             )
-            bank = next_bank([P, n // P, P], f"ta{a}_{j0}")
-            blocks = n // P
-            for b in range(blocks):
-                nc.tensor.matmul(bank[:, b, :], h[a][:, j0 + b * P : j0 + (b + 1) * P], ident[:],
-                                 start=(b == 0), stop=False, is_transpose=True)
-            for b in range(blocks):
-                nc.tensor.matmul(bank[:, b, :], g[:, b * P : (b + 1) * P], ident[:],
-                                 start=False, stop=(b == blocks - 1), is_transpose=True)
+            gt[a, j0] = (g, n)
+
+        def th(a, j0, n, b, d=0):
+            bank = bank_tile([P, 512], f"ta{a}_{j0}", b)
+            if d:
+                dummy(bank, d)
+            ta[a, j0] = bank
+            for c in range(n // P):
+                nc.tensor.matmul(bank[:, c * P : (c + 1) * P], h[a][:, j0 + c * P : j0 + (c + 1) * P], ident[:],
+                                 start=(c == 0), stop=False, is_transpose=True)
+
+        def tg(a, j0):
+            g, n = gt[a, j0]
+            bank = ta[a, j0]
+            for c in range(n // P):
+                nc.tensor.matmul(bank[:, c * P : (c + 1) * P], g[:, c * P : (c + 1) * P], ident[:],
+                                 start=False, stop=(c == n // P - 1), is_transpose=True)
+
+        def zcopy(a, j0, e):
+            g, n = gt[a, j0]
+            bank = ta[a, j0]
             for k, (g0, gn) in enumerate(GROUPS):
                 if j0 <= g0 < j0 + n:
-                    b0 = (g0 - j0) // P
-                    nc.scalar.copy(
+                    ENG[e](
                         zt[k][:, :, :, 64 * a : 64 * (a + 1)],
-                        bank[:, b0 : b0 + gn // P, :].rearrange("p b (u x) -> p b u x", u=2),
+                        bank[:, g0 - j0 : g0 - j0 + gn].rearrange("p (b u x) -> p b u x", u=2, x=64),
                     )
 
-        def turn_back(k, copy):
-            n = GROUPS[k][1]
-            words = zt[k][:].rearrange("p b u x -> p (b u x)").bitcast(F32)
-            bk = next_bank([P, 2, n], f"bk{k}")
-            for b in range(n // P):
-                for u in range(2):
-                    w0 = (2 * b + u) * P
-                    nc.tensor.transpose(bk[:, u, b * P : (b + 1) * P], words[:, w0 : w0 + P], ident[:])
-            zq = keep.tile([P, n * PACK], BF16, name=f"zq{k}", align_bytes=64)
-            copy(zq[:].bitcast(F32).rearrange("p (j u) -> p j u", u=2), bk[:].rearrange("p u j -> p j u"))
-            return zq
+        def tz(a, j0, e):
+            tg(a, j0)
+            zcopy(a, j0, e)
 
-        def layer2(k, zq, copy):
-            j0, n = GROUPS[k]
-            zc = keep.tile([P, n], U32, name=f"zc{k}", align_bytes=64)
-            zs = keep.tile([P, n], U8, name=f"zs{k}", align_bytes=64)
-            nc.vector.quantize_mx(out=zc[:].bitcast(FP8X4), scales=zs[:], in_=zq[:])
-            acc = next_bank([P, n], f"res{k}")
+        def piece(a, j0, n, b, e):
+            gath(a, j0, n)
+            th(a, j0, n, b)
+            tz(a, j0, e)
+
+        def dummy(bank, n):
             nc.tensor.matmul_mx(
-                out=acc[:], lhsT=w2_codes[:].bitcast(FP8X4), lhsT_scale=w2_scales[:],
+                out=bank[:, :n], lhsT=w1c[0, 0].bitcast(FP8X4), lhsT_scale=w1s[0, 0],
+                rhs=gw0[:, :n].bitcast(FP8X4), rhs_scale=gs[:, :n], start=True, stop=True,
+            )
+
+        def back(k, b, e, d=0):
+            g0, n = GROUPS[k]
+            j0 = max(u for u, un in UNITS if u <= g0)
+            dst = zq[j0][:, (g0 - j0) * PACK : (g0 - j0 + n) * PACK]
+            words = zt[k][:].rearrange("p b u x -> p (b u x)").bitcast(F32)
+            full = bank_tile([P, 512], f"bk{k}", b)
+            if d:
+                dummy(full, d)
+            bk = full[:, : 2 * n].rearrange("p (u j) -> p u j", u=2)
+            for c in range(n // P):
+                for u in range(2):
+                    w0 = (2 * c + u) * P
+                    nc.tensor.transpose(bk[:, u, c * P : (c + 1) * P], words[:, w0 : w0 + P], ident[:])
+            ENG[e](dst.bitcast(F32).rearrange("p (j u) -> p j u", u=2), bk.rearrange("p u j -> p j u"))
+
+        def qz(i):
+            j0, n = UNITS[i]
+            zc = sb([P, n], U32, f"zc{j0}")
+            zs = sb([P, n], U8, f"zs{j0}")
+            nc.vector.quantize_mx(out=zc[:].bitcast(FP8X4), scales=zs[:], in_=zq[j0][:])
+            zcs[i] = (zc, zs)
+
+        def mo(i, b, e):
+            j0, n = UNITS[i]
+            zc, zs = zcs[i]
+            res = bank_tile([P, n], f"res{j0}", b)
+            nc.tensor.matmul_mx(
+                out=res[:], lhsT=w2q["c"][:].bitcast(FP8X4), lhsT_scale=w2q["s"][:],
                 rhs=zc[:].bitcast(FP8X4), rhs_scale=zs[:], start=True, stop=True,
             )
-            res = keep.tile([P, n], F32, name=f"o{k}")
-            copy(res[:], acc[:])
-            nc.sync.dma_start(out=out[:, j0 : j0 + n], in_=res[:])
+            o = sb([P, n], F32, f"o{j0}")
+            ENG[e](o[:], res[:])
+            nc.sync.dma_start(out=out[:, j0 : j0 + n], in_=o[:])
 
-        prep_w1(1, nc.scalar.copy)
-        layer1(0)
-        layer1(1)
-        prep_w1(2, nc.vector.tensor_copy)
-        layer1(2)
-        prep_w1(3, nc.vector.tensor_copy)
-        layer1(3)
-        prep_w2()
-        turn[0] = 6
-        zq = []
-        for hf in range(2):
-            for a in range(PLANES - 1):
-                piece(a, hf * HALF, HALF)
-            mine = [k for k, (j0, n) in enumerate(GROUPS) if j0 // HALF == hf]
-            for k in mine:
-                piece(PLANES - 1, *GROUPS[k])
-            for k in mine:
-                zq.append(turn_back(k, nc.scalar.copy))
-        for k in range(len(GROUPS)):
-            layer2(k, zq[k], nc.vector.tensor_copy)
+        def finish(i, b, e):
+            qz(i)
+            mo(i, b, e)
+
+        nc.vector.tensor_copy(gs[:], xs[:].indirect(offs_t[:]))
+        nc.vector.tensor_copy(gw0[:], xw[0][:].bitcast(U32).indirect(offs_t[:]))
+        cast_w1(0, 0)
+        quant_w1(0, 0)
+        gather_x1(0)
+        cast_w1(0, 1)
+        quant_w1(0, 1)
+        gather_x1(1)
+        gather_x1(2)
+        mm1(0, 0, 0)
+        relu(0, 0, "S")
+        mm1(0, 1, 1)
+        relu(0, 1, "S")
+        mm1(0, 2, 2)
+        relu(0, 2, "S")
+        cast_w1(1, 0)
+        cast_w1(1, 1)
+        quant_w1(1, 0)
+        mm1(1, 0, 3)
+        relu(1, 0, "S")
+        mm1pair(1, 4)
+        relu(1, 1, "S")
+        cast_w1(2, 0)
+        cast_w1(2, 1)
+        quant_w1(2, 0)
+        cast_w2()
+        quant_w2()
+        th(0, 0, 512, 5)
+        gath(0, 0, 512)
+        cast_w1(3, 0)
+        cast_w1(3, 1)
+        th(1, 0, 512, 0)
+        th(0, 512, 512, 3)
+        tz(0, 0, "S")
+        mm1(2, 0, 6)
+        mm1pair(2, 7)
+        relu(2, 0, "S")
+        relu(2, 1, "S")
+        gath(1, 0, 512)
+        quant_w1(3, 0)
+        tg(1, 0)
+        mm1(3, 0, 1)
+        mm1pair(3, 2)
+        relu(3, 0, "S")
+        relu(3, 1, "S")
+        zcopy(1, 0, "S")
+        gath(0, 512, 512)
+        th(2, 0, 512, 4)
+        tz(0, 512, "S")
+        gath(2, 0, 512)
+        th(3, 0, 256, 6, 512)
+        th(3, 256, 256, 7)
+        tz(2, 0, "S")
+        th(1, 512, 256, 5)
+        gath(3, 0, 256)
+        tz(3, 0, "S")
+        gath(3, 256, 256)
+        th(2, 512, 256, 0, 512)
+        tz(3, 256, "S")
+        th(3, 512, 256, 1)
+        back(0, 2, "S")
+        gath(1, 512, 256)
+        tz(1, 512, "S")
+        back(1, 3, "S")
+        gath(2, 512, 256)
+        tz(2, 512, "S")
+        gath(3, 512, 256)
+        th(1, 768, 256, 4, 512)
+        tz(3, 512, "S")
+        th(2, 768, 256, 6)
+        th(3, 768, 128, 7)
+        th(3, 896, 128, 5)
+        gath(1, 768, 256)
+        tz(1, 768, "S")
+        gath(2, 768, 256)
+        tz(2, 768, "S")
+        back(2, 2, "S")
+        gath(3, 768, 128)
+        gath(3, 896, 128)
+        tz(3, 768, "V")
+        tz(3, 896, "V")
+        qz(0)
+        qz(1)
+        back(3, 1, "S", 0)
+        back(4, 3, "V")
+        mo(0, 0, "S")
+        mo(1, 4, "S")
+        qz(2)
+        qz(3)
+        qz(4)
+        mo(2, 6, "S")
+        mo(3, 7, "V")
+        mo(4, 5, "V")

@@ -15,372 +15,321 @@ U8 = mybir.dt.uint8
 FP8X4 = mybir.dt.float8_e4m3fn_x4
 RELU = mybir.ActivationFunctionType.Relu
 MULT = mybir.AluOpType.mult
-MAX = mybir.AluOpType.max
 
 P = 128
 PACK = 4
-PASSES = K // (P * PACK)
+K_PASS = P * PACK
+PASSES = K // K_PASS
 PLANES = H // P
-HALF = S // 2
+LIST = 16
+QUADRANT = 32
+BANK = 512
 BANKS = 8
-GROUPS = [(0, 256), (256, 256), (512, 256), (768, 128), (896, 128)]
-UNITS = [(0, 256), (256, 256), (512, 256), (768, 128), (896, 128)]
-LOADS = [(0,1),(1,1),(2,1),(3,1)]
-ORDER = "x0 w00 x1 w01 w10 w11 r w20 w21 v w30 w31"
-GW1 = [(0, 512), (512, 256), (768, 256)]
-CAST = "SS SS VV SS V"
-TAGS = {"gw11": "wb01", "wb3": "g2", "zc0": "g3", "zc256": "g2"}
-GRING = 4
+HALF = S // 2
+QUARTER = S // 4
+PER_ROW = S // P
+RING = 4
+
+X_SLICES = [(0, HALF), (HALF, QUARTER), (HALF + QUARTER, QUARTER)]
+Z_TURNS = [(0, QUARTER), (QUARTER, QUARTER), (HALF, QUARTER), (S - 2 * P, P), (S - P, P)]
+Z_UNITS = [(0, HALF), (HALF, QUARTER), (S - 2 * P, P), (S - P, P)]
 
 
 def tile_picked_treeup_relu_p_kernel(
     tc, x_words, x_scales, w1, w2, share, offs, par, out
 ):
     nc = tc.nc
+    on_scalar, on_vector = nc.scalar.copy, nc.vector.tensor_copy
     with ExitStack() as ctx:
         keep = ctx.enter_context(tc.tile_pool(name="keep", bufs=1))
         psum = ctx.enter_context(tc.psum_pool(name="psum", bufs=1))
-        made = [0]
 
-        def bank_tile(shape, name, b):
-            return psum.tile(shape, F32, name=name, tag=f"bank{b}")
+        def sbuf(shape, dtype, name, tag=None):
+            return keep.tile(shape, dtype, name=name, align_bytes=64, tag=tag or name)
 
-        def sb(shape, dtype, name):
-            return keep.tile(shape, dtype, name=name, align_bytes=64, tag=TAGS.get(name, name))
+        free_banks = list(range(BANKS))
+        bank_of = {}
 
-        offs_t = keep.tile([P, S // 16], U16, name="offs_t")
-        par_t = keep.tile([P, S // 16], U16, name="par_t")
-        xs = keep.tile([P, T], U8, name="xs", align_bytes=64)
-        xw = [keep.tile([P, T], I32, name=f"xw{z}", align_bytes=64) for z in range(PASSES)]
-        w1_raw = {(a0, z): keep.tile([P, PACK, P * na], F32, name=f"w1r{a0}{z}", align_bytes=64)
-                  for a0, na in LOADS for z in range(PASSES)}
-        w2_raw = keep.tile([P, PACK, N], F32, name="w2_raw", align_bytes=64)
+        def take_bank(width, name):
+            bank_of[name] = free_banks[0]
+            free_banks.remove(bank_of[name])
+            return psum.tile([P, width], F32, name=name, tag=f"bank{bank_of[name]}")
+
+        def give_bank(name):
+            free_banks.append(bank_of[name])
+
+        offs_t = keep.tile([P, S // LIST], U16, name="offs_t")
+        par_t = keep.tile([P, S // LIST], U16, name="par_t")
+        x_scale_rows = sbuf([P, T], U8, "x_scale_rows")
+        x_table = [sbuf([P, T], I32, f"x_table{z}") for z in range(PASSES)]
+        w1_raw = {(a, z): sbuf([P, PACK, P], F32, f"w1_raw{a}{z}") for a in range(PLANES) for z in range(PASSES)}
+        w2_raw = sbuf([P, PACK, N], F32, "w2_raw")
+        share_col = keep.tile([P, PER_ROW], F32, name="share_col")
         ident = keep.tile([P, P], F32, name="ident")
-        warm = keep.tile([P, 8], F32, name="warm")
-
-        def load_w1(k, z):
-            a0, na = LOADS[k]
-            rows = w1[z * 512 : (z + 1) * 512, a0 * P : (a0 + na) * P]
-            nc.sync.dma_start(out=w1_raw[a0, z][:], in_=rows.rearrange("(p t) c -> p t c", t=PACK))
+        table_warm = keep.tile([P, 1], F32, name="table_warm")
 
         def load_x(z):
-            nc.sync.dma_start(out=xw[z][:], in_=x_words[z].rearrange("p c r -> p (c r)").bitcast(I32))
+            nc.sync.dma_start(out=x_table[z][:], in_=x_words[z].rearrange("p c r -> p (c r)").bitcast(I32))
 
-        def load_w2():
-            nc.sync.dma_start(out=w2_raw[:], in_=w2.rearrange("(p t) m -> p t m", t=PACK))
+        def load_w1(a, z):
+            rows = w1[z * K_PASS : (z + 1) * K_PASS, a * P : (a + 1) * P]
+            nc.sync.dma_start(out=w1_raw[a, z][:], in_=rows.rearrange("(p t) c -> p t c", t=PACK))
 
-        def load_scales():
-            for q in range(4):
-                nc.sync.dma_start(
-                    out=xs[32 * q : 32 * q + 8, :].bitcast(I32),
-                    in_=x_scales[:, 4 * q : 4 * q + 4, :].bitcast(I32),
-                )
-
-        nc.gpsimd.memset(xs[:].bitcast(I32), 0)
-        scol = keep.tile([P, 8], F32, name="scol")
+        nc.gpsimd.memset(x_scale_rows[:].bitcast(I32), 0)
         nc.sync.dma_start(offs_t[:], offs)
-        if "r" in ORDER.split():
-            nc.sync.dma_start(out=scol[:], in_=share[0, :].rearrange("(p e) -> p e", e=8))
-        else:
-            nc.sync.dma_start(par_t[:], par)
-        load_scales()
-        for w in ORDER.split():
-            if w[0] == "x":
-                load_x(int(w[1]))
-            elif w[0] == "w":
-                load_w1(int(w[1]), int(w[2]))
-            elif w[0] == "r":
-                nc.sync.dma_start(par_t[:], par)
-            else:
-                load_w2()
+        nc.sync.dma_start(out=share_col[:], in_=share[0, :].rearrange("(p e) -> p e", e=PER_ROW))
+        for q in range(P // QUADRANT):
+            nc.sync.dma_start(
+                out=x_scale_rows[QUADRANT * q : QUADRANT * q + PASSES * PACK, :].bitcast(I32),
+                in_=x_scales[:, PACK * q : PACK * (q + 1), :].bitcast(I32),
+            )
+        for z in range(PASSES):
+            load_x(z)
+            load_w1(0, z)
+        for z in range(PASSES):
+            load_w1(1, z)
+        nc.sync.dma_start(par_t[:], par)
+        for z in range(PASSES):
+            load_w1(2, z)
+        nc.sync.dma_start(out=w2_raw[:], in_=w2.rearrange("(p t) m -> p t m", t=PACK))
+        for z in range(PASSES):
+            load_w1(3, z)
 
         make_identity(nc, ident[:])
-        nc.scalar.activation(warm[:, 0:1], ident[:, 0:1], RELU)
-        ENG = {"S": nc.scalar.copy, "V": nc.vector.tensor_copy}
-        casts = CAST.split()
+        nc.scalar.activation(table_warm[:], ident[:, 0:1], RELU)
 
-        if "r" in ORDER.split():
-            whole = keep.tile([P, S], F32, name="share_w")
-            share_t = [whole[:, :HALF], whole[:, HALF:]]
-            for hf in range(2):
-                bank = bank_tile([P, HALF], f"sB{hf}", 5 + hf)
-                for c in range(4):
-                    b = 4 * hf + c
-                    nc.tensor.transpose(bank[:, c * P : (c + 1) * P], scol[:, b : b + 1].to_broadcast([P, P]), ident[:])
-                nc.scalar.copy(whole[:].rearrange("p (n e) -> p n e", e=8)[:, :, 4 * hf : 4 * hf + 4], bank[:].rearrange("p (e n) -> p n e", e=4))
-        gs = sb([P, S], U8, "gs")
-        gw0 = sb([P, S], U32, "gw0")
-        gw1 = {}
-        wb = {}
-        w1c = {}
-        w1s = {}
-        h = {}
-        acc = {}
-        zt = [sb([P, n // P, 2, 2 * P], BF16, f"zt{j0}") for j0, n in GROUPS]
-        zq = {j0: sb([P, n * PACK], BF16, f"zq{j0}") for j0, n in UNITS}
-        w2q = {}
+        share_t = keep.tile([P, S], F32, name="share_t")
+        per_bank = BANK // P
+        for e0 in range(0, PER_ROW, per_bank):
+            spread = take_bank(BANK, f"spread{e0}")
+            for e in range(per_bank):
+                nc.tensor.transpose(
+                    spread[:, e * P : (e + 1) * P], share_col[:, e0 + e : e0 + e + 1].to_broadcast([P, P]), ident[:]
+                )
+            on_scalar(
+                share_t[:].rearrange("p (n e) -> p n e", e=PER_ROW)[:, :, e0 : e0 + per_bank],
+                spread[:].rearrange("p (e n) -> p n e", e=per_bank),
+            )
+            give_bank(f"spread{e0}")
 
-        def gather_x1(i):
-            j0, n = GW1[i]
-            gw1[i] = sb([P, n], U32, f"gw1{i}")
-            nc.vector.tensor_copy(gw1[i][:], xw[1][:].bitcast(U32).indirect(offs_t[:, j0 // 16 : (j0 + n) // 16]))
+        x_scale = sbuf([P, S], U8, "x_scale")
+        x_pass0 = sbuf([P, S], U32, "x_pass0")
+        x_pass1 = {}
+        w1_bf, w1_codes, w1_scales = {}, {}, {}
+        h, acc = {}, {}
 
-        def cast_w1(a, z):
-            a0 = max(b for b, na in LOADS if b <= a)
-            if a == 0:
-                wb[a, z] = sb([P, 512], BF16, f"wb{a}{z}")[:]
-            else:
-                if z == 0:
-                    wb[a] = sb([P, 1024], BF16, f"wb{a}")
-                wb[a, z] = wb[a][:, z * 512 : (z + 1) * 512]
-            ENG[casts[a][z]](
-                wb[a, z].rearrange("p (u m e t) -> p m t u e", u=2, m=32, e=2, t=PACK),
-                w1_raw[a0, z][:, :, (a - a0) * P : (a - a0 + 1) * P].rearrange("p t (m u e) -> p m t u e", m=32, u=2, e=2),
+        def gather_pass1(i, tag=None):
+            j0, n = X_SLICES[i]
+            x_pass1[i] = sbuf([P, n], U32, f"x_pass1_{i}", tag)
+            nc.vector.tensor_copy(
+                x_pass1[i][:], x_table[1][:].bitcast(U32).indirect(offs_t[:, j0 // LIST : (j0 + n) // LIST])
             )
 
-        def quant_w1(a, z):
-            if a == 0:
-                c = sb([P, P], U32, f"w1c{a}{z}")
-                s = sb([P, P], U8, f"w1s{a}{z}")
-                nc.vector.quantize_mx(out=c[:].bitcast(FP8X4), scales=s[:], in_=wb[a, z])
-                w1c[a, z], w1s[a, z] = c[:], s[:]
-            else:
-                c = sb([P, 2 * P], U32, f"w1c{a}")
-                s = sb([P, 2 * P], U8, f"w1s{a}")
-                nc.vector.quantize_mx(out=c[:].bitcast(FP8X4), scales=s[:], in_=wb[a][:])
-                for y in range(2):
-                    w1c[a, y], w1s[a, y] = c[:, y * P : (y + 1) * P], s[:, y * P : (y + 1) * P]
+        def cast_w1(a, z, dst, copy):
+            copy(
+                dst.rearrange("p (u m e t) -> p m t u e", u=2, m=P // PACK, e=2, t=PACK),
+                w1_raw[a, z][:].rearrange("p t (m u e) -> p m t u e", m=P // PACK, u=2, e=2),
+            )
 
-        def mm1(a, i, b):
-            j0, n = GW1[i]
-            acc[a, i] = bank_tile([P, n], f"acc{a}{i}", b)
+        def cast_plane(a, copy, tag=None):
+            w1_bf[a] = sbuf([P, PASSES * K_PASS], BF16, f"w1_bf{a}", tag)
             for z in range(PASSES):
-                rhs = gw0[:, j0 : j0 + n] if z == 0 else gw1[i][:]
-                nc.tensor.matmul_mx(
-                    out=acc[a, i][:], lhsT=w1c[a, z].bitcast(FP8X4), lhsT_scale=w1s[a, z],
-                    rhs=rhs.bitcast(FP8X4), rhs_scale=gs[4 * z : P, j0 : j0 + n],
-                    start=(z == 0), stop=(z == PASSES - 1),
+                cast_w1(a, z, w1_bf[a][:, z * K_PASS : (z + 1) * K_PASS], copy)
+
+        def quantise(src, name, tag=None):
+            words = src.shape[1] // PACK
+            codes = sbuf([P, words], U32, f"{name}_codes", tag)
+            scales = sbuf([P, words], U8, f"{name}_scales")
+            nc.vector.quantize_mx(out=codes[:].bitcast(FP8X4), scales=scales[:], in_=src)
+            return codes, scales
+
+        def quantise_plane(a):
+            codes, scales = quantise(w1_bf[a][:], f"w1_{a}")
+            for z in range(PASSES):
+                w1_codes[a, z], w1_scales[a, z] = codes[:, z * P : (z + 1) * P], scales[:, z * P : (z + 1) * P]
+
+        def layer1(a, slices):
+            j_first = X_SLICES[slices[0]][0]
+            bank = take_bank(sum(X_SLICES[i][1] for i in slices), f"acc{a}_{j_first}")
+            acc[a, j_first] = bank
+            for i in slices:
+                j0, n = X_SLICES[i]
+                for z in range(PASSES):
+                    nc.tensor.matmul_mx(
+                        out=bank[:, j0 - j_first : j0 - j_first + n],
+                        lhsT=w1_codes[a, z].bitcast(FP8X4),
+                        lhsT_scale=w1_scales[a, z],
+                        rhs=(x_pass0[:, j0 : j0 + n] if z == 0 else x_pass1[i][:]).bitcast(FP8X4),
+                        rhs_scale=x_scale[PACK * z : P, j0 : j0 + n],
+                        start=(z == 0),
+                        stop=(z == PASSES - 1),
+                    )
+
+        def relu(a, j0):
+            if a not in h:
+                h[a] = sbuf([P, S], F32, f"h{a}")
+            nc.scalar.activation(h[a][:, j0 : j0 + acc[a, j0].shape[1]], acc[a, j0][:], RELU)
+            give_bank(f"acc{a}_{j0}")
+
+        def layer1_plane(a):
+            layer1(a, [0])
+            layer1(a, [1, 2])
+            relu(a, 0)
+            relu(a, HALF)
+
+        z_t = [sbuf([P, n // P, 2, 2 * P], BF16, f"z_t{j0}") for j0, n in Z_TURNS]
+        z_in = {j0: sbuf([P, n * PACK], BF16, f"z_in{j0}") for j0, n in Z_UNITS}
+        gathered, sums = {}, {}
+
+        def ring_tag(k):
+            return f"ring{k % RING}"
+
+        def gather_h(a, j0, n):
+            g = sbuf([P, n], F32, f"g{a}_{j0}", ring_tag(len(gathered)))
+            nc.vector.tensor_tensor(
+                g[:], h[a][:].indirect(par_t[:, j0 // LIST : (j0 + n) // LIST]), share_t[:, j0 : j0 + n], MULT
+            )
+            gathered[a, j0] = g
+
+        def open_sum(planes, j0, n):
+            bank = take_bank(BANK, f"sum{planes[0]}_{j0}")
+            for i, a in enumerate(planes):
+                sums[a, j0] = (bank, planes, n)
+                for c in range(0, n, P):
+                    nc.tensor.matmul(
+                        bank[:, i * n + c : i * n + c + P], h[a][:, j0 + c : j0 + c + P], ident[:],
+                        start=(i == 0 and c == 0), stop=False, is_transpose=True,
+                    )
+
+        def add_gathered(a, j0):
+            bank, planes, n = sums[a, j0]
+            i = planes.index(a)
+            for c in range(0, n, P):
+                nc.tensor.matmul(
+                    bank[:, i * n + c : i * n + c + P], gathered[a, j0][:, c : c + P], ident[:],
+                    start=False, stop=(a == planes[-1] and c == n - P), is_transpose=True,
                 )
 
-        def mm1pair(a, b):
-            bk = bank_tile([P, HALF], f"acc{a}1", b)
-            for i in (1, 2):
-                j0, n = GW1[i]
-                for z in range(PASSES):
-                    rhs = gw0[:, j0 : j0 + n] if z == 0 else gw1[i][:]
-                    nc.tensor.matmul_mx(
-                        out=bk[:, j0 - HALF : j0 - HALF + n], lhsT=w1c[a, z].bitcast(FP8X4), lhsT_scale=w1s[a, z],
-                        rhs=rhs.bitcast(FP8X4), rhs_scale=gs[4 * z : P, j0 : j0 + n],
-                        start=(z == 0), stop=(z == PASSES - 1),
+        def round_sum(a, j0, copy):
+            bank, planes, n = sums[a, j0]
+            count = len(planes)
+            for k, (t0, tn) in enumerate(Z_TURNS):
+                if j0 <= t0 < j0 + n:
+                    src = bank[:, : count * n].rearrange("p (i j) -> p i j", i=count)[:, :, t0 - j0 : t0 - j0 + tn]
+                    copy(
+                        z_t[k][:, :, :, 64 * planes[0] : 64 * (planes[-1] + 1)].rearrange("p b u (i x) -> p i b u x", i=count),
+                        src.rearrange("p i (b u x) -> p i b u x", u=2, x=64),
                     )
-            acc[a, 1] = bk
+            give_bank(f"sum{planes[0]}_{j0}")
 
-        def relu(a, i, e):
-            if a not in h:
-                h[a] = sb([P, S], F32, f"h{a}")
-            j0 = GW1[i][0]
-            n = acc[a, i].shape[1]
-            if e == "S":
-                nc.scalar.activation(h[a][:, j0 : j0 + n], acc[a, i][:], RELU)
-            else:
-                nc.vector.tensor_scalar(h[a][:, j0 : j0 + n], acc[a, i][:], 0.0, None, MAX)
+        def close_sum(a, j0, copy):
+            add_gathered(a, j0)
+            round_sum(a, j0, copy)
 
-        def cast_w2():
-            w2q["b"] = sb([P, N * PACK], BF16, "w2b")
-            ENG[casts[4]](
-                w2q["b"][:].rearrange("p (c i t) -> p c t i", i=4, t=PACK),
-                w2_raw[:].rearrange("p t (c i) -> p c t i", i=4),
-            )
-
-        def quant_w2():
-            w2q["c"] = sb([P, N], U32, "w2c")
-            w2q["s"] = sb([P, N], U8, "w2s")
-            nc.vector.quantize_mx(out=w2q["c"][:].bitcast(FP8X4), scales=w2q["s"][:], in_=w2q["b"][:])
-
-        gt = {}
-        ta = {}
-        bks = {}
-        zcs = {}
-        ress = {}
-
-        def gath(a, j0, n):
-            g = keep.tile([P, n], F32, name=f"g{a}_{j0}", align_bytes=64, tag=TAGS.get(f"g{a}_{j0}", f"g{made[0] % GRING}"))
-            made[0] = made[0] + 1
-            nc.vector.tensor_tensor(
-                g[:], h[a][:].indirect(par_t[:, j0 // 16 : (j0 + n) // 16]),
-                share_t[j0 // HALF][:, j0 % HALF : j0 % HALF + n], MULT
-            )
-            gt[a, j0] = (g, n)
-
-        def th(a, j0, n, b, d=0):
-            bank = bank_tile([P, 512], f"ta{a}_{j0}", b)
-            if d:
-                dummy(bank, d)
-            ta[a, j0] = bank
-            for c in range(n // P):
-                nc.tensor.matmul(bank[:, c * P : (c + 1) * P], h[a][:, j0 + c * P : j0 + (c + 1) * P], ident[:],
-                                 start=(c == 0), stop=False, is_transpose=True)
-
-        def tg(a, j0):
-            g, n = gt[a, j0]
-            bank = ta[a, j0]
-            for c in range(n // P):
-                nc.tensor.matmul(bank[:, c * P : (c + 1) * P], g[:, c * P : (c + 1) * P], ident[:],
-                                 start=False, stop=(c == n // P - 1), is_transpose=True)
-
-        def zcopy(a, j0, e):
-            g, n = gt[a, j0]
-            bank = ta[a, j0]
-            for k, (g0, gn) in enumerate(GROUPS):
-                if j0 <= g0 < j0 + n:
-                    ENG[e](
-                        zt[k][:, :, :, 64 * a : 64 * (a + 1)],
-                        bank[:, g0 - j0 : g0 - j0 + gn].rearrange("p (b u x) -> p b u x", u=2, x=64),
-                    )
-
-        def tz(a, j0, e):
-            tg(a, j0)
-            zcopy(a, j0, e)
-
-        def piece(a, j0, n, b, e):
-            gath(a, j0, n)
-            th(a, j0, n, b)
-            tz(a, j0, e)
-
-        def dummy(bank, n):
-            nc.tensor.matmul_mx(
-                out=bank[:, :n], lhsT=w1c[0, 0].bitcast(FP8X4), lhsT_scale=w1s[0, 0],
-                rhs=gw0[:, :n].bitcast(FP8X4), rhs_scale=gs[:, :n], start=True, stop=True,
-            )
-
-        def back(k, b, e, d=0):
-            g0, n = GROUPS[k]
-            j0 = max(u for u, un in UNITS if u <= g0)
-            dst = zq[j0][:, (g0 - j0) * PACK : (g0 - j0 + n) * PACK]
-            words = zt[k][:].rearrange("p b u x -> p (b u x)").bitcast(F32)
-            full = bank_tile([P, 512], f"bk{k}", b)
-            if d:
-                dummy(full, d)
-            bk = full[:, : 2 * n].rearrange("p (u j) -> p u j", u=2)
-            for c in range(n // P):
+        def turn_back(k, copy):
+            t0, n = Z_TURNS[k]
+            j0 = max(u0 for u0, un in Z_UNITS if u0 <= t0)
+            words = z_t[k][:].rearrange("p b u x -> p (b u x)").bitcast(F32)
+            bank = take_bank(BANK, f"back{k}")
+            runs = bank[:, : 2 * n].rearrange("p (u j) -> p u j", u=2)
+            for b in range(n // P):
                 for u in range(2):
-                    w0 = (2 * c + u) * P
-                    nc.tensor.transpose(bk[:, u, c * P : (c + 1) * P], words[:, w0 : w0 + P], ident[:])
-            ENG[e](dst.bitcast(F32).rearrange("p (j u) -> p j u", u=2), bk.rearrange("p u j -> p j u"))
+                    w0 = (2 * b + u) * P
+                    nc.tensor.transpose(runs[:, u, b * P : (b + 1) * P], words[:, w0 : w0 + P], ident[:])
+            dst = z_in[j0][:, (t0 - j0) * PACK : (t0 - j0 + n) * PACK]
+            copy(dst.bitcast(F32).rearrange("p (j u) -> p j u", u=2), runs.rearrange("p u j -> p j u"))
+            give_bank(f"back{k}")
 
-        def qz(i):
-            j0, n = UNITS[i]
-            zc = sb([P, n], U32, f"zc{j0}")
-            zs = sb([P, n], U8, f"zs{j0}")
-            nc.vector.quantize_mx(out=zc[:].bitcast(FP8X4), scales=zs[:], in_=zq[j0][:])
-            zcs[i] = (zc, zs)
-
-        def mo(i, b, e):
-            j0, n = UNITS[i]
-            zc, zs = zcs[i]
-            res = bank_tile([P, n], f"res{j0}", b)
+        def layer2(i, z_mx, w2_mx, copy):
+            j0, n = Z_UNITS[i]
+            bank = take_bank(n, f"res{j0}")
             nc.tensor.matmul_mx(
-                out=res[:], lhsT=w2q["c"][:].bitcast(FP8X4), lhsT_scale=w2q["s"][:],
-                rhs=zc[:].bitcast(FP8X4), rhs_scale=zs[:], start=True, stop=True,
+                out=bank[:], lhsT=w2_mx[0][:].bitcast(FP8X4), lhsT_scale=w2_mx[1][:],
+                rhs=z_mx[0][:].bitcast(FP8X4), rhs_scale=z_mx[1][:], start=True, stop=True,
             )
-            o = sb([P, n], F32, f"o{j0}")
-            ENG[e](o[:], res[:])
-            nc.sync.dma_start(out=out[:, j0 : j0 + n], in_=o[:])
+            result = sbuf([P, n], F32, f"result{j0}")
+            copy(result[:], bank[:])
+            give_bank(f"res{j0}")
+            nc.sync.dma_start(out=out[:, j0 : j0 + n], in_=result[:])
 
-        def finish(i, b, e):
-            qz(i)
-            mo(i, b, e)
+        nc.vector.tensor_copy(x_scale[:], x_scale_rows[:].indirect(offs_t[:]))
+        nc.vector.tensor_copy(x_pass0[:], x_table[0][:].bitcast(U32).indirect(offs_t[:]))
+        for z in range(PASSES):
+            first = sbuf([P, K_PASS], BF16, f"w1_bf0{z}")
+            cast_w1(0, z, first[:], on_scalar)
+            codes, scales = quantise(first[:], f"w1_0{z}")
+            w1_codes[0, z], w1_scales[0, z] = codes[:], scales[:]
+            gather_pass1(z, "w1_bf01" if z == 1 else None)
+        gather_pass1(2)
+        for i, (j0, n) in enumerate(X_SLICES):
+            layer1(0, [i])
+            relu(0, j0)
 
-        nc.vector.tensor_copy(gs[:], xs[:].indirect(offs_t[:]))
-        nc.vector.tensor_copy(gw0[:], xw[0][:].bitcast(U32).indirect(offs_t[:]))
-        cast_w1(0, 0)
-        quant_w1(0, 0)
-        gather_x1(0)
-        cast_w1(0, 1)
-        quant_w1(0, 1)
-        gather_x1(1)
-        gather_x1(2)
-        mm1(0, 0, 0)
-        relu(0, 0, "S")
-        mm1(0, 1, 1)
-        relu(0, 1, "S")
-        mm1(0, 2, 2)
-        relu(0, 2, "S")
-        cast_w1(1, 0)
-        cast_w1(1, 1)
-        quant_w1(1, 0)
-        mm1(1, 0, 3)
-        relu(1, 0, "S")
-        mm1pair(1, 4)
-        relu(1, 1, "S")
-        cast_w1(2, 0)
-        cast_w1(2, 1)
-        quant_w1(2, 0)
-        cast_w2()
-        quant_w2()
-        th(0, 0, 512, 5)
-        gath(0, 0, 512)
-        cast_w1(3, 0)
-        cast_w1(3, 1)
-        th(1, 0, 512, 0)
-        th(0, 512, 512, 3)
-        tz(0, 0, "S")
-        mm1(2, 0, 6)
-        mm1pair(2, 7)
-        relu(2, 0, "S")
-        relu(2, 1, "S")
-        gath(1, 0, 512)
-        quant_w1(3, 0)
-        tg(1, 0)
-        mm1(3, 0, 1)
-        mm1pair(3, 2)
-        relu(3, 0, "S")
-        relu(3, 1, "S")
-        zcopy(1, 0, "S")
-        gath(0, 512, 512)
-        th(2, 0, 512, 4)
-        tz(0, 512, "S")
-        gath(2, 0, 512)
-        th(3, 0, 256, 6, 512)
-        th(3, 256, 256, 7)
-        tz(2, 0, "S")
-        th(1, 512, 256, 5)
-        gath(3, 0, 256)
-        tz(3, 0, "S")
-        gath(3, 256, 256)
-        th(2, 512, 256, 0, 512)
-        tz(3, 256, "S")
-        th(3, 512, 256, 1)
-        back(0, 2, "S")
-        gath(1, 512, 256)
-        tz(1, 512, "S")
-        back(1, 3, "S")
-        gath(2, 512, 256)
-        tz(2, 512, "S")
-        gath(3, 512, 256)
-        th(1, 768, 256, 4, 512)
-        tz(3, 512, "S")
-        th(2, 768, 256, 6)
-        th(3, 768, 128, 7)
-        th(3, 896, 128, 5)
-        gath(1, 768, 256)
-        tz(1, 768, "S")
-        gath(2, 768, 256)
-        tz(2, 768, "S")
-        back(2, 2, "S")
-        gath(3, 768, 128)
-        gath(3, 896, 128)
-        tz(3, 768, "V")
-        tz(3, 896, "V")
-        qz(0)
-        qz(1)
-        back(3, 1, "S", 0)
-        back(4, 3, "V")
-        mo(0, 0, "S")
-        mo(1, 4, "S")
-        qz(2)
-        qz(3)
-        qz(4)
-        mo(2, 6, "S")
-        mo(3, 7, "V")
-        mo(4, 5, "V")
+        cast_plane(1, on_scalar)
+        quantise_plane(1)
+        layer1(1, [0])
+        relu(1, 0)
+        layer1(1, [1, 2])
+        relu(1, HALF)
+        cast_plane(2, on_vector)
+        quantise_plane(2)
+        w2_bf = sbuf([P, N * PACK], BF16, "w2_bf")
+        on_vector(
+            w2_bf[:].rearrange("p (c i t) -> p c t i", i=4, t=PACK),
+            w2_raw[:].rearrange("p t (c i) -> p c t i", i=4),
+        )
+        w2_mx = quantise(w2_bf[:], "w2")
+
+        open_sum([0], 0, HALF)
+        gather_h(0, 0, HALF)
+        cast_plane(3, on_scalar, ring_tag(2))
+        open_sum([1], 0, HALF)
+        open_sum([0], HALF, HALF)
+        close_sum(0, 0, on_scalar)
+        layer1_plane(2)
+        gather_h(1, 0, HALF)
+        quantise_plane(3)
+        add_gathered(1, 0)
+        layer1_plane(3)
+        round_sum(1, 0, on_scalar)
+        gather_h(0, HALF, HALF)
+        open_sum([2], 0, HALF)
+        close_sum(0, HALF, on_scalar)
+
+        for j0 in (HALF, HALF + QUARTER):
+            open_sum([1, 2], j0, QUARTER)
+        gather_h(2, 0, HALF)
+        open_sum([3], 0, QUARTER)
+        close_sum(2, 0, on_scalar)
+        open_sum([3], QUARTER, QUARTER)
+        open_sum([3], HALF, QUARTER)
+        gather_h(3, 0, QUARTER)
+        close_sum(3, 0, on_scalar)
+        for j0, n in Z_TURNS[-2:]:
+            open_sum([3], j0, n)
+        gather_h(3, QUARTER, QUARTER)
+        close_sum(3, QUARTER, on_scalar)
+
+        for k, j0 in enumerate((HALF, HALF + QUARTER)):
+            turn_back(k, on_scalar)
+            for a in (1, 2):
+                gather_h(a, j0, QUARTER)
+                add_gathered(a, j0)
+            round_sum(2, j0, on_scalar)
+            if k == 0:
+                gather_h(3, j0, QUARTER)
+                close_sum(3, j0, on_scalar)
+        for j0, n in Z_TURNS[-2:]:
+            gather_h(3, j0, n)
+
+        for j0, n in Z_TURNS[-2:]:
+            close_sum(3, j0, on_vector)
+        turn_back(2, on_scalar)
+        z_mx = [quantise(z_in[0][:], "z0", ring_tag(len(gathered) - 2))]
+        turn_back(3, on_vector)
+        turn_back(4, on_vector)
+        layer2(0, z_mx[0], w2_mx, on_scalar)
+        for j0, n in Z_UNITS[1:]:
+            z_mx.append(quantise(z_in[j0][:], f"z{j0}"))
+        for i, copy in ((1, on_scalar), (2, on_scalar), (3, on_vector)):
+            layer2(i, z_mx[i], w2_mx, copy)

@@ -29,6 +29,7 @@ HALF = S // 2
 QUARTER = S // 4
 PER_ROW = S // P
 RING = 4
+RUN = P // 2
 
 X_SLICES = [(0, HALF), (HALF, QUARTER), (HALF + QUARTER, QUARTER)]
 Z_TURNS = [(0, QUARTER), (QUARTER, QUARTER), (HALF, QUARTER), (S - 2 * P, P), (S - P, P)]
@@ -66,7 +67,6 @@ def tile_picked_treeup_relu_p_kernel(
         w2_raw = sbuf([P, PACK, N], F32, "w2_raw")
         share_col = keep.tile([P, PER_ROW], F32, name="share_col")
         ident = keep.tile([P, P], F32, name="ident")
-        table_warm = keep.tile([P, 1], F32, name="table_warm")
 
         def load_x(z):
             nc.sync.dma_start(out=x_table[z][:], in_=x_words[z].rearrange("p c r -> p (c r)").bitcast(I32))
@@ -96,7 +96,6 @@ def tile_picked_treeup_relu_p_kernel(
             load_w1(3, z)
 
         make_identity(nc, ident[:])
-        nc.scalar.activation(table_warm[:], ident[:, 0:1], RELU)
 
         share_t = keep.tile([P, S], F32, name="share_t")
         per_bank = BANK // P
@@ -148,6 +147,12 @@ def tile_picked_treeup_relu_p_kernel(
             for z in range(PASSES):
                 w1_codes[a, z], w1_scales[a, z] = codes[:, z * P : (z + 1) * P], scales[:, z * P : (z + 1) * P]
 
+        def prepare_plane0(z):
+            cast = sbuf([P, K_PASS], BF16, f"w1_bf0{z}")
+            cast_w1(0, z, cast[:], on_scalar)
+            codes, scales = quantise(cast[:], f"w1_0{z}")
+            w1_codes[0, z], w1_scales[0, z] = codes[:], scales[:]
+
         def layer1(a, slices):
             j_first = X_SLICES[slices[0]][0]
             bank = take_bank(sum(X_SLICES[i][1] for i in slices), f"acc{a}_{j_first}")
@@ -177,7 +182,7 @@ def tile_picked_treeup_relu_p_kernel(
             relu(a, 0)
             relu(a, HALF)
 
-        z_t = [sbuf([P, n // P, 2, 2 * P], BF16, f"z_t{j0}") for j0, n in Z_TURNS]
+        z_t = [sbuf([P, n // P, 2, PLANES * RUN], BF16, f"z_t{j0}") for j0, n in Z_TURNS]
         z_in = {j0: sbuf([P, n * PACK], BF16, f"z_in{j0}") for j0, n in Z_UNITS}
         gathered, sums = {}, {}
 
@@ -217,8 +222,8 @@ def tile_picked_treeup_relu_p_kernel(
                 if j0 <= t0 < j0 + n:
                     src = bank[:, : count * n].rearrange("p (i j) -> p i j", i=count)[:, :, t0 - j0 : t0 - j0 + tn]
                     copy(
-                        z_t[k][:, :, :, 64 * planes[0] : 64 * (planes[-1] + 1)].rearrange("p b u (i x) -> p i b u x", i=count),
-                        src.rearrange("p i (b u x) -> p i b u x", u=2, x=64),
+                        z_t[k][:, :, :, RUN * planes[0] : RUN * (planes[-1] + 1)].rearrange("p b u (i x) -> p i b u x", i=count),
+                        src.rearrange("p i (b u x) -> p i b u x", u=2, x=RUN),
                     )
             give_bank(f"sum{planes[0]}_{j0}")
 
@@ -254,12 +259,10 @@ def tile_picked_treeup_relu_p_kernel(
 
         nc.vector.tensor_copy(x_scale[:], x_scale_rows[:].indirect(offs_t[:]))
         nc.vector.tensor_copy(x_pass0[:], x_table[0][:].bitcast(U32).indirect(offs_t[:]))
-        for z in range(PASSES):
-            first = sbuf([P, K_PASS], BF16, f"w1_bf0{z}")
-            cast_w1(0, z, first[:], on_scalar)
-            codes, scales = quantise(first[:], f"w1_0{z}")
-            w1_codes[0, z], w1_scales[0, z] = codes[:], scales[:]
-            gather_pass1(z, "w1_bf01" if z == 1 else None)
+        prepare_plane0(0)
+        gather_pass1(0)
+        prepare_plane0(1)
+        gather_pass1(1, "w1_bf01")
         gather_pass1(2)
         for i, (j0, n) in enumerate(X_SLICES):
             layer1(0, [i])
@@ -275,8 +278,8 @@ def tile_picked_treeup_relu_p_kernel(
         quantise_plane(2)
         w2_bf = sbuf([P, N * PACK], BF16, "w2_bf")
         on_vector(
-            w2_bf[:].rearrange("p (c i t) -> p c t i", i=4, t=PACK),
-            w2_raw[:].rearrange("p t (c i) -> p c t i", i=4),
+            w2_bf[:].rearrange("p (c n t) -> p c t n", n=4, t=PACK),
+            w2_raw[:].rearrange("p t (c n) -> p c t n", n=4),
         )
         w2_mx = quantise(w2_bf[:], "w2")
 

from contextlib import ExitStack

import concourse.mybir as mybir
from concourse.masks import make_identity

K, T, S, H, N = 1024, 2048, 1024, 512, 128
FLOPS = 2 * K * H * S + 2 * H * N * S

F32 = mybir.dt.float32
BF16 = mybir.dt.bfloat16
I32 = mybir.dt.int32
U32 = mybir.dt.uint32
U16 = mybir.dt.uint16
U8 = mybir.dt.uint8
FP8X4 = mybir.dt.float8_e4m3fn_x4
RELU = mybir.ActivationFunctionType.Relu
MULT = mybir.AluOpType.mult

P = 128
PACK = 4
K_PASS = P * PACK
PASSES = K // K_PASS
PLANES = H // P
LIST = 16
QUADRANT = 32
BANK = 512
BANKS = 8
HALF = S // 2
QUARTER = S // 4
PER_ROW = S // P
RING = 4
RUN = P // 2

X_SLICES = [(0, HALF), (HALF, QUARTER), (HALF + QUARTER, QUARTER)]
Z_TURNS = [(0, QUARTER), (QUARTER, QUARTER), (HALF, QUARTER), (S - 2 * P, P), (S - P, P)]
Z_UNITS = [(0, HALF), (HALF, QUARTER), (S - 2 * P, P), (S - P, P)]


def tile_picked_treeup_relu_p_kernel(
    tc, x_words, x_scales, w1, w2, share, offs, par, out
):
    nc = tc.nc
    on_scalar, on_vector = nc.scalar.copy, nc.vector.tensor_copy
    with ExitStack() as ctx:
        keep = ctx.enter_context(tc.tile_pool(name="keep", bufs=1))
        psum = ctx.enter_context(tc.psum_pool(name="psum", bufs=1))

        def sbuf(shape, dtype, name, tag=None):
            return keep.tile(shape, dtype, name=name, align_bytes=64, tag=tag or name)

        free_banks = list(range(BANKS))
        bank_of = {}

        def take_bank(width, name):
            bank_of[name] = free_banks[0]
            free_banks.remove(bank_of[name])
            return psum.tile([P, width], F32, name=name, tag=f"bank{bank_of[name]}")

        def give_bank(name):
            free_banks.append(bank_of[name])

        offs_t = keep.tile([P, S // LIST], U16, name="offs_t")
        par_t = keep.tile([P, S // LIST], U16, name="par_t")
        x_scale_rows = sbuf([P, T], U8, "x_scale_rows")
        x_table = [sbuf([P, T], I32, f"x_table{z}") for z in range(PASSES)]
        w1_raw = {(a, z): sbuf([P, PACK, P], F32, f"w1_raw{a}{z}") for a in range(PLANES) for z in range(PASSES)}
        w2_raw = sbuf([P, PACK, N], F32, "w2_raw")
        share_col = keep.tile([P, PER_ROW], F32, name="share_col")
        ident = keep.tile([P, P], F32, name="ident")

        def load_x(z):
            nc.sync.dma_start(out=x_table[z][:], in_=x_words[z].rearrange("p c r -> p (c r)").bitcast(I32))

        def load_w1(a, z):
            rows = w1[z * K_PASS : (z + 1) * K_PASS, a * P : (a + 1) * P]
            nc.sync.dma_start(out=w1_raw[a, z][:], in_=rows.rearrange("(p t) c -> p t c", t=PACK))

        nc.gpsimd.memset(x_scale_rows[:].bitcast(I32), 0)
        nc.sync.dma_start(offs_t[:], offs)
        nc.sync.dma_start(out=share_col[:], in_=share[0, :].rearrange("(p e) -> p e", e=PER_ROW))
        for q in range(P // QUADRANT):
            nc.sync.dma_start(
                out=x_scale_rows[QUADRANT * q : QUADRANT * q + PASSES * PACK, :].bitcast(I32),
                in_=x_scales[:, PACK * q : PACK * (q + 1), :].bitcast(I32),
            )
        for z in range(PASSES):
            load_x(z)
            load_w1(0, z)
        for z in range(PASSES):
            load_w1(1, z)
        nc.sync.dma_start(par_t[:], par)
        for z in range(PASSES):
            load_w1(2, z)
        nc.sync.dma_start(out=w2_raw[:], in_=w2.rearrange("(p t) m -> p t m", t=PACK))
        for z in range(PASSES):
            load_w1(3, z)

        make_identity(nc, ident[:])

        share_t = keep.tile([P, S], F32, name="share_t")
        per_bank = BANK // P
        for e0 in range(0, PER_ROW, per_bank):
            spread = take_bank(BANK, f"spread{e0}")
            for e in range(per_bank):
                nc.tensor.transpose(
                    spread[:, e * P : (e + 1) * P], share_col[:, e0 + e : e0 + e + 1].to_broadcast([P, P]), ident[:]
                )
            on_scalar(
                share_t[:].rearrange("p (n e) -> p n e", e=PER_ROW)[:, :, e0 : e0 + per_bank],
                spread[:].rearrange("p (e n) -> p n e", e=per_bank),
            )
            give_bank(f"spread{e0}")

        x_scale = sbuf([P, S], U8, "x_scale")
        x_pass0 = sbuf([P, S], U32, "x_pass0")
        x_pass1 = {}
        w1_bf, w1_codes, w1_scales = {}, {}, {}
        h, acc = {}, {}

        def gather_pass1(i, tag=None):
            j0, n = X_SLICES[i]
            x_pass1[i] = sbuf([P, n], U32, f"x_pass1_{i}", tag)
            nc.vector.tensor_copy(
                x_pass1[i][:], x_table[1][:].bitcast(U32).indirect(offs_t[:, j0 // LIST : (j0 + n) // LIST])
            )

        def cast_w1(a, z, dst, copy):
            copy(
                dst.rearrange("p (u m e t) -> p m t u e", u=2, m=P // PACK, e=2, t=PACK),
                w1_raw[a, z][:].rearrange("p t (m u e) -> p m t u e", m=P // PACK, u=2, e=2),
            )

        def cast_plane(a, copy, tag=None):
            w1_bf[a] = sbuf([P, PASSES * K_PASS], BF16, f"w1_bf{a}", tag)
            for z in range(PASSES):
                cast_w1(a, z, w1_bf[a][:, z * K_PASS : (z + 1) * K_PASS], copy)

        def quantise(src, name, tag=None):
            words = src.shape[1] // PACK
            codes = sbuf([P, words], U32, f"{name}_codes", tag)
            scales = sbuf([P, words], U8, f"{name}_scales")
            nc.vector.quantize_mx(out=codes[:].bitcast(FP8X4), scales=scales[:], in_=src)
            return codes, scales

        def quantise_plane(a):
            codes, scales = quantise(w1_bf[a][:], f"w1_{a}")
            for z in range(PASSES):
                w1_codes[a, z], w1_scales[a, z] = codes[:, z * P : (z + 1) * P], scales[:, z * P : (z + 1) * P]

        def prepare_plane0(z):
            cast = sbuf([P, K_PASS], BF16, f"w1_bf0{z}")
            cast_w1(0, z, cast[:], on_scalar)
            codes, scales = quantise(cast[:], f"w1_0{z}")
            w1_codes[0, z], w1_scales[0, z] = codes[:], scales[:]

        def layer1(a, slices):
            j_first = X_SLICES[slices[0]][0]
            bank = take_bank(sum(X_SLICES[i][1] for i in slices), f"acc{a}_{j_first}")
            acc[a, j_first] = bank
            for i in slices:
                j0, n = X_SLICES[i]
                for z in range(PASSES):
                    nc.tensor.matmul_mx(
                        out=bank[:, j0 - j_first : j0 - j_first + n],
                        lhsT=w1_codes[a, z].bitcast(FP8X4),
                        lhsT_scale=w1_scales[a, z],
                        rhs=(x_pass0[:, j0 : j0 + n] if z == 0 else x_pass1[i][:]).bitcast(FP8X4),
                        rhs_scale=x_scale[PACK * z : P, j0 : j0 + n],
                        start=(z == 0),
                        stop=(z == PASSES - 1),
                    )

        def relu(a, j0):
            if a not in h:
                h[a] = sbuf([P, S], F32, f"h{a}")
            nc.scalar.activation(h[a][:, j0 : j0 + acc[a, j0].shape[1]], acc[a, j0][:], RELU)
            give_bank(f"acc{a}_{j0}")

        def layer1_plane(a):
            layer1(a, [0])
            layer1(a, [1, 2])
            relu(a, 0)
            relu(a, HALF)

        z_t = [sbuf([P, n // P, 2, PLANES * RUN], BF16, f"z_t{j0}") for j0, n in Z_TURNS]
        z_in = {j0: sbuf([P, n * PACK], BF16, f"z_in{j0}") for j0, n in Z_UNITS}
        gathered, sums = {}, {}

        def ring_tag(k):
            return f"ring{k % RING}"

        def gather_h(a, j0, n):
            g = sbuf([P, n], F32, f"g{a}_{j0}", ring_tag(len(gathered)))
            nc.vector.tensor_tensor(
                g[:], h[a][:].indirect(par_t[:, j0 // LIST : (j0 + n) // LIST]), share_t[:, j0 : j0 + n], MULT
            )
            gathered[a, j0] = g

        def open_sum(planes, j0, n):
            bank = take_bank(BANK, f"sum{planes[0]}_{j0}")
            for i, a in enumerate(planes):
                sums[a, j0] = (bank, planes, n)
                for c in range(0, n, P):
                    nc.tensor.matmul(
                        bank[:, i * n + c : i * n + c + P], h[a][:, j0 + c : j0 + c + P], ident[:],
                        start=(i == 0 and c == 0), stop=False, is_transpose=True,
                    )

        def add_gathered(a, j0):
            bank, planes, n = sums[a, j0]
            i = planes.index(a)
            for c in range(0, n, P):
                nc.tensor.matmul(
                    bank[:, i * n + c : i * n + c + P], gathered[a, j0][:, c : c + P], ident[:],
                    start=False, stop=(a == planes[-1] and c == n - P), is_transpose=True,
                )

        def round_sum(a, j0, copy):
            bank, planes, n = sums[a, j0]
            count = len(planes)
            for k, (t0, tn) in enumerate(Z_TURNS):
                if j0 <= t0 < j0 + n:
                    src = bank[:, : count * n].rearrange("p (i j) -> p i j", i=count)[:, :, t0 - j0 : t0 - j0 + tn]
                    copy(
                        z_t[k][:, :, :, RUN * planes[0] : RUN * (planes[-1] + 1)].rearrange("p b u (i x) -> p i b u x", i=count),
                        src.rearrange("p i (b u x) -> p i b u x", u=2, x=RUN),
                    )
            give_bank(f"sum{planes[0]}_{j0}")

        def close_sum(a, j0, copy):
            add_gathered(a, j0)
            round_sum(a, j0, copy)

        def turn_back(k, copy):
            t0, n = Z_TURNS[k]
            j0 = max(u0 for u0, un in Z_UNITS if u0 <= t0)
            words = z_t[k][:].rearrange("p b u x -> p (b u x)").bitcast(F32)
            bank = take_bank(BANK, f"back{k}")
            runs = bank[:, : 2 * n].rearrange("p (u j) -> p u j", u=2)
            for b in range(n // P):
                for u in range(2):
                    w0 = (2 * b + u) * P
                    nc.tensor.transpose(runs[:, u, b * P : (b + 1) * P], words[:, w0 : w0 + P], ident[:])
            dst = z_in[j0][:, (t0 - j0) * PACK : (t0 - j0 + n) * PACK]
            copy(dst.bitcast(F32).rearrange("p (j u) -> p j u", u=2), runs.rearrange("p u j -> p j u"))
            give_bank(f"back{k}")

        def layer2(i, z_mx, w2_mx, copy):
            j0, n = Z_UNITS[i]
            bank = take_bank(n, f"res{j0}")
            nc.tensor.matmul_mx(
                out=bank[:], lhsT=w2_mx[0][:].bitcast(FP8X4), lhsT_scale=w2_mx[1][:],
                rhs=z_mx[0][:].bitcast(FP8X4), rhs_scale=z_mx[1][:], start=True, stop=True,
            )
            result = sbuf([P, n], F32, f"result{j0}")
            copy(result[:], bank[:])
            give_bank(f"res{j0}")
            nc.sync.dma_start(out=out[:, j0 : j0 + n], in_=result[:])

        nc.vector.tensor_copy(x_scale[:], x_scale_rows[:].indirect(offs_t[:]))
        nc.vector.tensor_copy(x_pass0[:], x_table[0][:].bitcast(U32).indirect(offs_t[:]))
        prepare_plane0(0)
        gather_pass1(0)
        prepare_plane0(1)
        gather_pass1(1, "w1_bf01")
        gather_pass1(2)
        for i, (j0, n) in enumerate(X_SLICES):
            layer1(0, [i])
            relu(0, j0)

        cast_plane(1, on_scalar)
        quantise_plane(1)
        layer1(1, [0])
        relu(1, 0)
        layer1(1, [1, 2])
        relu(1, HALF)
        cast_plane(2, on_vector)
        quantise_plane(2)
        w2_bf = sbuf([P, N * PACK], BF16, "w2_bf")
        on_vector(
            w2_bf[:].rearrange("p (c n t) -> p c t n", n=4, t=PACK),
            w2_raw[:].rearrange("p t (c n) -> p c t n", n=4),
        )
        w2_mx = quantise(w2_bf[:], "w2")

        open_sum([0], 0, HALF)
        gather_h(0, 0, HALF)
        cast_plane(3, on_scalar, ring_tag(2))
        open_sum([1], 0, HALF)
        open_sum([0], HALF, HALF)
        close_sum(0, 0, on_scalar)
        layer1_plane(2)
        gather_h(1, 0, HALF)
        quantise_plane(3)
        add_gathered(1, 0)
        layer1_plane(3)
        round_sum(1, 0, on_scalar)
        gather_h(0, HALF, HALF)
        open_sum([2], 0, HALF)
        close_sum(0, HALF, on_scalar)

        for j0 in (HALF, HALF + QUARTER):
            open_sum([1, 2], j0, QUARTER)
        gather_h(2, 0, HALF)
        open_sum([3], 0, QUARTER)
        close_sum(2, 0, on_scalar)
        open_sum([3], QUARTER, QUARTER)
        open_sum([3], HALF, QUARTER)
        gather_h(3, 0, QUARTER)
        close_sum(3, 0, on_scalar)
        for j0, n in Z_TURNS[-2:]:
            open_sum([3], j0, n)
        gather_h(3, QUARTER, QUARTER)
        close_sum(3, QUARTER, on_scalar)

        for k, j0 in enumerate((HALF, HALF + QUARTER)):
            turn_back(k, on_scalar)
            for a in (1, 2):
                gather_h(a, j0, QUARTER)
                add_gathered(a, j0)
            round_sum(2, j0, on_scalar)
            if k == 0:
                gather_h(3, j0, QUARTER)
                close_sum(3, j0, on_scalar)
        for j0, n in Z_TURNS[-2:]:
            gather_h(3, j0, n)

        for j0, n in Z_TURNS[-2:]:
            close_sum(3, j0, on_vector)
        turn_back(2, on_scalar)
        z_mx = [quantise(z_in[0][:], "z0", ring_tag(len(gathered) - 2))]
        turn_back(3, on_vector)
        turn_back(4, on_vector)
        layer2(0, z_mx[0], w2_mx, on_scalar)
        for j0, n in Z_UNITS[1:]:
            z_mx.append(quantise(z_in[j0][:], f"z{j0}"))
        for i, copy in ((1, on_scalar), (2, on_scalar), (3, on_vector)):
            layer2(i, z_mx[i], w2_mx, copy)
